import numpy as np, ml_dtypes
CORES = [66,74,82,90,194,202,210,218]
N = 8
BF = ml_dtypes.bfloat16
W, SV, M, HOPS = 4096, 256, 160, [1, 4, 2]
RO = len(HOPS) + 1
def names(rng, power, *shape):
    return np.minimum((W * rng.random(shape) ** power).astype(np.int64), W - 1)
def pairs(rng, C, power):
    a = names(rng, power, N, 8, 16, C); b = np.take_along_axis(a, np.argsort(rng.random((N, 8, 16, C)), axis=2), 2)
    share = rng.choice(np.array([0.0, 0.15, 0.5, 1.0]), (N, 8, 1, C)); b = np.where(rng.random(b.shape) < share, b, names(rng, power, N, 8, 16, C))
    fa = rng.choice(np.array([0.05, 0.12, 0.3, 0.7, 1.0]), (N, 8, 1, C), p=[0.2, 0.25, 0.2, 0.2, 0.15])
    fb = rng.choice(np.array([0.0, 0.3, 0.7, 1.0]), (N, 8, 1, C), p=[0.05, 0.25, 0.3, 0.4])
    return np.where(rng.random(a.shape) < fa, a, -1), np.where(rng.random(b.shape) < fb, b, -1)
def parts(rng, power):
    clk = rng.integers(0, 256, (N, 8, 16, W)); z = rng.integers(0, 256, (N, 8, 16, M)); th = rng.integers(1200, 1600, (N, 8))
    sc, st = pairs(rng, SV, power); d, t = pairs(rng, M, power)
    return clk, sc, st, d, t, z, th
def pack(clk, sc, st, d, t, z, th):
    return {"clk": clk.reshape(N, 128, W).astype(np.float32).astype(BF), "sc": sc.reshape(N, 128, SV).astype(np.int32), "st": st.reshape(N, 128, SV).astype(np.int32),
            "dl": d.reshape(N, 128, M).astype(np.int32), "tl": t.reshape(N, 128, M).astype(np.int32), "z0": z.reshape(N, 128, M).astype(np.float32).astype(BF),
            "th": np.repeat(th.reshape(N, 8), 16, axis=1).reshape(N, 128, 1).astype(np.int32)}
def setup_inputs(rng):
    return pack(*parts(rng, 1))
def setup_inputs_spread(rng):
    clk, sc, st, d, t, z, th = parts(rng, 4)
    clk = np.floor(np.exp2(8 * rng.random((N, 8, 1, W))) * rng.random((N, 8, 16, W))).astype(np.int64)
    z = np.floor(np.exp2(8 * rng.random((N, 8, 1, M))) * rng.random((N, 8, 16, M))).astype(np.int64)
    th = np.minimum(np.floor(np.exp2(12 * rng.random((N, 8)))).astype(np.int64), 4080)
    return pack(np.minimum(clk, 255), sc, st, d, t, np.minimum(z, 255), th)
def setup_inputs_ends(rng):
    def rec(C):
        p = rng.choice(np.array([0.0, 0.06, 0.5, 1.0]), (N, 8, 1, C)); s = (N, 8, 16, C)
        a = np.where(rng.random(s) < p, W - 1, -1)
        o = np.where(rng.random(s) < 0.3, -1, np.where(rng.random(s) < 0.15, W - 1, rng.integers(0, W, s)))
        return np.where(rng.random((N, 8, 1, C)) < 0.6, a, o)
    def half(C):
        k = rng.integers(0, 3, (N, 8, 1, C))
        return np.where(k == 0, 0, np.where(k == 1, 255, 255 * rng.integers(0, 2, (N, 8, 16, C))))
    clk = half(W); z = half(M); sc = rec(SV); st = rec(SV); d = rec(M); t = rec(M)
    g = np.arange(8)[None, :]; q = np.arange(N)[:, None]
    clk[..., 0] = 255; clk[..., W - 1] = np.where(((g + q + N) & 1) == 0, 255, 0)[:, :, None]
    clk[..., W - 2] = 255; clk[:, :, 15, W - 2] = 254
    z[..., 0] = 255; z[..., M - 1] = 255; z[..., M - 2] = 0
    th = 4080 * ((g // 2 + q + rng.integers(0, 2, (N, 1))) & 1); th[:, 5] = 4080
    for m, lo, hi in ((M - 1, 0, W - 1), (0, W - 1, 0)):
        d[..., m] = -1; d[:, :, 15, m] = W - 1; d[:, :, 4, m] = 5; t[..., m] = -1; t[:, :, 2, m] = lo; t[:, :, 15, m] = hi
    s = slice(M - 6, M - 2); z[..., s] = 255; d[:, :, 15, s] = W - 1; t[..., s] = -1; t[:, :, 2, s] = W - 2; t[:, :, 15, s] = 0
    d[:, 5] = W - 1; t[:, 5] = W - 1; sc[:, 5] = W - 1; st[:, 5] = W - 1; z[:, 5] = z[:, 5, :1]
    return pack(clk, sc, st, d, t, z, th)
def setup_inputs_corners(rng):
    clk, sc, st, d, t, z, th = parts(rng, 1)
    clk[:, 1::2, :, 1::2] = clk[:, 1::2, :, 0::2]
    th = rng.choice(np.array([0, 1, 126, 128, 1000, 1999, 4080]), (N, 8)); th[:, 0] = 1000; th[:, 7] = 1999; th[:, 3] = 0
    th[:, 5] = 2051 + 4 * rng.integers(0, 100, N); th[:, 6] = 2052 + 4 * rng.integers(0, 100, N)
    lanes = np.array([0, 1, SV - 1, SV, W - 2, W - 1])
    for q in range(N):
        for g in range(8):
            kind = rng.permutation(M) % 10; n = np.where(rng.random(M) < 0.5, rng.choice(lanes, M), rng.integers(0, W, M)); full = rng.integers(0, W, (16, M))
            D = d[q, g]; T = t[q, g]; x = clk[q, g][:, n]; room = np.maximum(x, 255 - x)
            gap = np.maximum(int(th[q, g]) + rng.integers(-1, 2, M), 0); step = np.clip(gap[None, :] - (np.add.accumulate(room, axis=0) - room), 0, room)
            near = np.where(x < 128, x + step, x - step)
            s = kind == 0; D[:, s] = -1; T[:, s] = -1; T[15, s] = n[s]
            s = kind == 1; D[:, s] = -1; T[:, s] = -1
            s = kind == 2; D[:, s] = full[:, s]; T[:, s] = -1
            s = kind == 3; D[:, s] = full[:, s]; T[:, s] = full[::-1][:, s]
            s = kind == 4; D[:, s] = n[s]; T[:, s] = -1; T[15, s] = n[s]
            s = kind == 5; D[:, s] = full[:, s] & ~1; T[:, s] = full[::-1][:, s] | 1
            s = kind == 6; D[:, s] = -1; D[15, s] = n[s]; T[:, s] = -1; T[0, s] = n[s]
            s = kind == 7; D[:, s] = -1; D[0, s] = n[s]; T[:, s] = -1; T[15, s] = n[s] ^ 1
            s = kind == 8; D[:, s] = -1; D[7, s] = n[s]; D[8, s] = (n[s] + 5) % W; T[:, s] = -1; T[15, s] = n[s]; T[3, s] = n[s] ^ 1
            s = kind == 9; D[:, s] = n[s]; D[0, s] = n[s] ^ 1; T[:, s] = n[s]
            s = (kind == 4) | (kind == 6) | (kind == 8) | (kind == 9); z[q, g][:, s] = near[:, s]
    k = rng.integers(0, 6, (N, 8, 1, SV)); more = rng.integers(0, W, (2, N, 8, 16, SV))
    st = np.where(k == 4, sc[:, :, ::-1], st)
    sc = np.where((k == 0) | (k == 2), -1, np.where(k == 1, more[0], sc)); st = np.where((k == 0) | (k == 3), -1, np.where(k == 1, more[1], st))
    return pack(clk, sc, st, d, t, z, th)
def setup_inputs_crowd(rng):
    clk, sc, st, d, t, z, th = parts(rng, 1); h = SV >> 1
    def high(*shape):
        return h + rng.integers(0, h - 1, shape) + SV * rng.integers(0, W // SV, shape)
    for q in range(N):
        for g in (0, 1):
            keep = d[q, g, :, M - 1].copy(), z[q, g, :, M - 1].copy()
            z[q, g] = rng.permuted(np.repeat(rng.integers(0, 256, (16, 1)), M, axis=1), axis=0); t[q, g] = -1
            if g == 1: d[q, g, :, M - 1], z[q, g, :, M - 1] = keep; t[q, g, 15, M - 1] = W - 1
        for g in (2, 3):
            v = int(rng.choice(np.array([0, SV - 1, SV >> 1]))); n = v + SV * rng.integers(0, W // SV, (16, M))
            t[q, g] = np.where(rng.random((16, M)) < 0.5, n, -1); t[q, g, 9] = n[9]; d[q, g] = -1
            if g == 3: d[q, g, 15, M - 1] = (v + 1) % W
        for g in (6, 7):
            n = rng.integers(0, W, M); z[q, g] = clk[q, g][:, n]; t[q, g, 5] = n
            d[q, g] = -1; d[q, g, 15] = n
            if g == 7: d[q, g, 15, M - 1] = -1
    for g, c, lim in ((4, 20, 219), (5, 35, 212)):
        clk[:, g] = rng.integers(0, 8, (N, 16, W)); clk[:, g, :, W - 1] = c
        d[:, g] = high(N, 16, M); t[:, g] = rng.permuted(d[:, g], axis=1)
        sc[:, g, :, :h] = high(N, 16, h); st[:, g, :, :h] = rng.permuted(sc[:, g, :, :h], axis=1)
        z[:, g] = rng.integers(0, 7, (N, 16, M))
        for q in range(N):
            z[q, g, :, M - 1] = 6 + (np.arange(16) < 4 + q)
            b = (q + int(np.sum(HOPS[:-1]))) % N; sc[b, g, :, 100 + q] = W - 1; st[b, g, :, 100 + q] = W - 1
            th[(b + HOPS[-1]) % N, g] = lim - q
    d[:, 5, 15, 0] = -1
    return pack(clk, sc, st, d, t, z, th)
def check_inputs(d):
    bad = []
    for k, lo, hi in (("clk", 0, 255), ("z0", 0, 255), ("sc", -1, W - 1), ("st", -1, W - 1), ("dl", -1, W - 1), ("tl", -1, W - 1), ("th", 0, 4080)):
        a = np.asarray(d[k]).astype(np.float64)
        if not (np.min(a) >= lo and np.max(a) <= hi): bad.append("range of " + k)
        elif np.any(a != np.floor(a)): bad.append("whole numbers in " + k)
    h = np.asarray(d["th"]).reshape(-1, 16)
    if np.any(h != h[:, :1]): bad.append("th alike in a group")
    return bad
def reference(clk, sc, st, dl, tl, z0, th):
    X = clk.astype(np.float32).astype(np.int64).reshape(N, 8, 16, W); Z = z0.astype(np.float32).astype(np.int64).reshape(N, 8, 16, M)
    C = sc.astype(np.int64).reshape(N, 8, 16, SV); S = st.astype(np.int64).reshape(N, 8, 16, SV)
    D = dl.astype(np.int64).reshape(N, 8, 16, M); T = tl.astype(np.int64).reshape(N, 8, 16, M)
    base = th.astype(np.int64).reshape(N, 8, 16)[:, :, 0]; A = np.zeros((N, 8), np.int64); row = np.arange(16).reshape(1, 16, 1)
    for visit in range(RO):
        nd, nt, nz = [], [], []
        for a in range(N):
            d, t, z = D[a], T[a], Z[a]
            x = np.take_along_axis(X[a], np.maximum(d, 0).reshape(8, 1, 16 * M), 2).reshape(8, 16, 16, M)
            y = np.take_along_axis(X[a], np.maximum(t, 0).reshape(8, 1, 16 * M), 2).reshape(8, 16, 16, M)
            dist = np.sum(np.abs(x - z[:, :, None, :]), axis=1)
            score = np.where(t >= 0, np.sum(np.minimum(y, z[:, :, None, :]), axis=1), -1)
            ks = np.argmax(score, axis=1)
            has = np.any(t >= 0, axis=1); v = np.take_along_axis(t, ks[:, None, :], 1)[:, 0] & (SV - 1)
            eq = (d[:, :, None, :] == t[:, None, :, :]) & (d >= 0)[:, :, None, :]
            cd = np.any(eq, axis=2); ct = np.any(eq, axis=1)
            lim = base[a] + 8 * (A[a] & 31)
            abort = np.any(cd & (dist > lim[:, None, None]), axis=1)
            d1 = np.where(cd, -1, d); t1 = np.where(ct | (row == ks[:, None, :]), -1, t)
            left = np.any(d1 >= 0, axis=1); proof = has & ~abort & ~left; go = has & ~abort & left
            yk = np.take_along_axis(y, ks[:, None, None, :], 2)[:, :, 0]
            top = np.max(np.where((d1 >= 0)[:, None, :, :], x, 0), axis=2)
            cv = np.take_along_axis(C[a], v[:, None, :], 2); sv = np.take_along_axis(S[a], v[:, None, :], 2)
            u = np.sum(z, axis=1) & (SV - 1)
            cu = np.take_along_axis(C[a], u[:, None, :], 2); su = np.take_along_axis(S[a], u[:, None, :], 2)
            hd = np.any(cv[:, :, None, :] == d[:, None, :, :], axis=2); ht = np.any(sv[:, :, None, :] == t[:, None, :, :], axis=2)
            d2 = np.where((d1 < 0) & ~hd, cv, d1); t2 = np.where((t1 < 0) & ~ht, sv, t1)
            ab = abort[:, None, :]; on = go[:, None, :]
            nd.append(np.where(ab, cv, np.where(on, d2, cu))); nt.append(np.where(ab, sv, np.where(on, t2, su)))
            nz.append(np.where(ab, np.abs(z - yk), np.where(on, (yk + top) >> 1, z)))
            A[a] += np.sum(cd & ~ab, axis=(1, 2))
            for g in range(8):
                for m in np.nonzero(proof[g])[0]: C[a, g, :, v[g, m]] = t1[g, :, m]
        D, T, Z = np.stack(nd), np.stack(nt), np.stack(nz)
        if visit < RO - 1: D, T, Z = [np.roll(b, HOPS[visit], axis=0) for b in (D, T, Z)]
    return {"yd": D.reshape(N, 128, M).astype(np.float32), "yt": T.reshape(N, 128, M).astype(np.float32), "yz": Z.reshape(N, 128, M).astype(np.float32), "ys": C.reshape(N, 128, SV).astype(np.float32)}

@@ -1,0 +1,619 @@
+import numpy as np
+from concourse.mybir import AluOpType, ActivationFunctionType
+
+OP = AluOpType
+AF = ActivationFunctionType
+NH = 2
+n = 80
+NM = 160
+G16 = 16 * n
+VIS = 4
+CW = 4112
+EQ = "vvs"
+SEEDS = 24
+
+SCRATCH = {}
+_W = {}
+
+
+def _buf(name, cols, dtype, where="sbuf"):
+    SCRATCH[name] = (where, [128, cols], dtype)
+    _W[name] = where
+
+
+for _i in range(8):
+    _buf("p%d" % _i, 512, "float32", "psum")
+_buf("clkw", CW, "bfloat16")
+for _nm, _c in (("dli", NM), ("tli", NM), ("sci", 256), ("sti", 256), ("thi", 1)):
+    _buf(_nm, _c, "int32")
+_buf("zin", NM, "bfloat16")
+_buf("tf", 256, "float32")
+_buf("sct", 256 + NM, "float32")
+_buf("stt", 256, "float32")
+_buf("ic", NM, "int32"); _buf("ik", 1, "int32"); _buf("id4", NM, "int32"); _buf("im", NM, "int32")
+_buf("kf", 4, "float32"); _buf("kdi", 1, "int32"); _buf("kmi", 1, "int32"); _buf("K16", 16, "float32")
+for _nm in ("BD", "ID", "I4096", "N25", "NI", "HI", "N512", "N8192", "BDa", "BDr"):
+    _buf(_nm, 128, "bfloat16")
+_buf("BDf", 128, "float32"); _buf("R15f", 128, "float32")
+_buf("RR", 2048, "float16"); _buf("SS", 2048, "bfloat16"); _buf("bia", 10, "bfloat16")
+_buf("seg0", G16, "bfloat16"); _buf("segM", 2 * G16, "bfloat16"); _buf("segV", 96, "float32")
+_buf("LOW", NM, "bfloat16"); _buf("co", 10, "uint16"); _buf("DUM", 10, "float32"); _buf("dmi", 10, "int32")
+_buf("thc", 1, "float32"); _buf("lim", 1, "float32"); _buf("As", 1, "int32"); _buf("Am", 1, "int32"); _buf("ac", 2, "float32")
+_buf("t1s", NM, "float32"); _buf("pv", 10, "float32"); _buf("pvb", 10, "bfloat16")
+_buf("VBs", NM, "bfloat16"); _buf("VL", NM, "bfloat16"); _buf("eb", NM, "bfloat16"); _buf("el", 16 * 45, "bfloat16")
+_buf("lo", NM, "bfloat16"); _buf("l0", 10, "float32"); _buf("xa", 10, "float32"); _buf("sou", 10, "uint16")
+_buf("yso", 256, "float32"); _buf("fin", 480, "float32")
+for _h in range(NH):
+    for _t in range(VIS):
+        _buf("msg%d%d" % (_t, _h), 320, "float16")
+        if _t < VIS - 1:
+            _buf("out%d%d" % (_t, _h), 240, "float16")
+    for _nm, _c, _d in (("offT", n, "uint16"), ("off1", n, "uint16"), ("Y", G16, "bfloat16"), ("X", G16, "bfloat16"), ("mn", G16, "bfloat16"),
+                        ("eq", G16, "bfloat16"), ("ea", 480, "bfloat16"), ("ab", 2 * G16, "bfloat16"), ("sm", 2 * G16, "bfloat16"),
+                        ("tp", G16, "bfloat16"), ("bf", 1840, "bfloat16"), ("f3", 1104, "float32"), ("hf", 160, "float16"),
+                        ("li", 16, "int32"), ("uv", 10, "int32"), ("lu", 16, "uint16"), ("lf", 40, "float32")):
+        _buf(_nm + str(_h), _c, _d)
+
+SEMAPHORES = ["sv", "ss", "st_", "sg", "snd"] + ["ld%d" % i for i in range(7)] + ["arr%d%d" % (t, h) for t in range(1, VIS) for h in range(NH)] + ["wr0", "wr1"]
+
+
+def F(name, a=0, b=None, s=1):
+    if b is None:
+        b = SCRATCH[name][1][1]
+    return (name, a, b, s)
+
+
+def IND(win, off):
+    return ("IND", win, off)
+
+
+def _build():
+    ops = []
+
+    def add(q, call, args, reads, writes, cost, **kw):
+        d = {"q": q, "call": call, "args": args, "r": reads, "w": writes, "cost": cost, "id": len(ops)}
+        d.update(kw)
+        ops.append(d)
+
+    def rd(*refs):
+        res = []
+        for x in refs:
+            res += [x[1], x[2]] if x[0] == "IND" else [x]
+        return res
+
+    def wid(x):
+        return 16 * (x[2][2] - x[2][1]) if x[0] == "IND" else -(-(x[2] - x[1]) // x[3])
+
+    def two(x):
+        return SCRATCH[x[0]][2] in ("bfloat16", "float16", "uint16")
+
+    def ps(x):
+        return _W[x[0]] == "psum"
+
+    CY = 0.83
+
+    def vcost(out, ins, tt):
+        k = wid(out)
+        if any(x[0] == "IND" for x in ins):
+            return 50 + 1.56 * CY * k
+        if out[0] == "IND":
+            return 50 + 3.8 * CY * k
+        if tt:
+            k = k if any(ps(x) for x in ins) else 2 * k
+        elif all(two(x) for x in ins + [out]):
+            k = k / 2
+        return max(64, k) * CY
+
+    def TT(out, a, b, op):
+        add("v", "tt", (out, a, b, op), rd(a, b), [out], vcost(out, [a, b], True))
+
+    def TS(out, a, s1, op0, s2=None, op1=None):
+        sr = [x for x in (s1, s2) if isinstance(x, tuple)]
+        add("v", "ts", (out, a, s1, s2, op0, op1), rd(a) + sr, [out], vcost(out, [a], False))
+
+    def CP(out, a):
+        w = [out[1]] if out[0] == "IND" else [out]
+        add("v", "cp", (out, a), rd(a) + ([out[2]] if out[0] == "IND" else []), w, vcost(out, [a], False))
+
+    def MS(out, c):
+        add("v", "ms", (out, c), [], [out], max(64, wid(out) * (0.5 if two(out) else 1)) * CY)
+
+    def SC(out, d0, d1, init, op0, op1):
+        add("v", "sc", (out, d0, d1, init, op0, op1), [d0, d1], [out], vcost(out, [d0, d1], False))
+
+    def VT(out, a):
+        add("v", "vt", (out, a), [a], [out], vcost(out, [a], False))
+
+    def ACT(out, a, f, bias=0.0, scale=1.0, acc=None):
+        k = wid(out)
+        c = 65 + 1.56 * CY * k if a[0] == "IND" else max(64, k) * CY
+        add("s", "act", (out, a, f, bias, scale, acc), rd(a) + [x for x in (bias, scale) if isinstance(x, tuple)], [out] + ([acc] if acc else []), c)
+
+    def MM(lst, more=False, cont=False):
+        c = 0
+        for (o, l, r) in lst:
+            c += max(64, wid(r)) * 0.42 * (4 if SCRATCH[r[0]][2] == "float32" else 1)
+        reads = [x[1] for x in lst] + [x[2] for x in lst]
+        add("t", "mm", (lst, not cont, not more), reads, [x[0] for x in lst], c)
+
+    def LD(q, out, name, sem):
+        add(q, "ld", (out, name), [], [out], 50, dma=sem, lat=6000 if name == "clk" else 2500)
+
+    LD("y", F("tli"), "tl", "ld0")
+    LD("y", F("dli"), "dl", "ld1")
+    LD("y", F("zin"), "z0", "ld2")
+    LD("y", F("thi"), "th", "ld3")
+    LD("y", F("sci"), "sc", "ld4")
+    LD("y", F("sti"), "st", "ld5")
+    LD("s", F("clkw", 16, CW), "clk", "ld6")
+    add("g", "iota", (F("ik"), [[0, 1]], 0, 1), [], [F("ik")], 135)
+    add("g", "iota", (F("ic"), [[1, NM]], 0, 0), [], [F("ic")], 400)
+    add("g", "iota", (F("dmi"), [[16, 10]], 256, 0), [], [F("dmi")], 150)
+    MS(F("clkw", 0, 16), -1.0)
+    TS(F("kdi"), F("ik"), 4, OP.arith_shift_right)
+    TS(F("kmi"), F("ik"), 15, OP.bitwise_and)
+    CP(F("kf", 0, 1), F("ik"))
+    CP(F("kf", 1, 2), F("kdi"))
+    CP(F("kf", 2, 3), F("kmi"))
+    TS(F("id4"), F("ic"), 4, OP.arith_shift_right)
+    TS(F("BD"), F("id4", 0, 128), F("kf", 1, 2), OP.is_equal)
+    TS(F("K16"), F("ic", 0, 16), F("kf", 2, 3), OP.is_equal)
+    TS(F("ID"), F("ic", 0, 128), F("kf", 0, 1), OP.is_equal)
+    for q in range(16):
+        TS(F("RR", 128 * q, 128 * q + 128), F("BD"), F("K16", q, q + 1), OP.mult)
+    MS(F("SS"), 0.0)
+    for q in range(16):
+        ACT(F("SS", 129 * q, 128 * q + 128, 16), F("BD", q, 128, 16), AF.Copy)
+    for nm, src, c in (("I4096", "ID", 4096.0), ("NI", "ID", -1.0), ("HI", "ID", 0.5), ("N512", "ID", -512.0), ("N8192", "ID", -8192.0),
+                       ("N25", "ID", -33554432.0), ("BDa", "BD", -128.0), ("BDr", "BD", -34.0), ("BDf", "BD", 1.0)):
+        ACT(F(nm), F(src), AF.Copy, 0.0, c)
+    ACT(F("R15f"), F("BD"), AF.Copy, 0.0, F("K16", 15, 16))
+    MS(F("segV"), 1000000.0)
+    MS(F("segV", 0, 96, 16), -1000000.0)
+    MS(F("seg0"), 1.0)
+    MS(F("seg0", 0, G16, 16), 0.0)
+    MS(F("segM"), 0.0)
+    MS(F("segM", 0, 2 * G16, 16), 8192.0)
+    MS(F("bia"), 0.0)
+    MS(F("bia", 5, 10), -1.0 / 16)
+    for h in range(NH):
+        MS(F("f3%d" % h, 0, 96), 0.0)
+    CP(F("tf", 0, NM), F("tli"))
+    TS(F("t1s"), F("tf", 0, NM), 3.0, OP.mult)
+    TT(F("t1s"), F("t1s"), F("tf", 0, NM), OP.min)
+    for h in range(NH):
+        m = "msg0%d" % h
+        TS(F(m, n, 2 * n), F("t1s", h * n, h * n + n), -2047.0, OP.add)
+        TS(F(m, 0, n), F("dli", h * n, h * n + n), -2047.0, OP.add)
+        CP(F(m, 2 * n, 3 * n), F("zin", h * n, h * n + n))
+    CP(F("thc"), F("thi"))
+    TS(F("kf", 3, 4), F("kf", 2, 3), -1.0 / 16, OP.mult, 31.0 / 32, OP.add)
+    TT(F("thc"), F("thc"), F("kf", 3, 4), OP.add)
+    CP(F("lim"), F("thc"))
+    MS(F("As"), 0)
+    TS(F("sct", 0, 256), F("sci"), 1.0, OP.add)
+    MS(F("sct", 256, 256 + NM), 0.0)
+    CP(F("tf"), F("sti"))
+    TS(F("stt"), F("tf"), 3.0, OP.mult)
+    TT(F("stt"), F("stt"), F("tf"), OP.min)
+    TS(F("stt"), F("stt"), -2047.0, OP.add)
+    TS(F("im"), F("ic"), 15, OP.bitwise_and)
+    TS(F("LOW"), F("im"), F("kf", 2, 3), OP.is_ge, 1024.0, OP.mult)
+    CP(F("co"), F("ic", 0, 10))
+    TS(F("DUM"), F("dmi"), F("kf", 2, 3), OP.add)
+
+    def Rq(q):
+        return F("RR", 128 * q, 128 * q + 128)
+
+    def Sq(q):
+        return F("SS", 128 * q, 128 * q + 128)
+
+    CH = [list(range(0, 6)), list(range(6, 12)), list(range(12, 16))]
+
+    def visit(t, h):
+        last = t == VIS - 1
+        H = str(h)
+        m = "msg%d%d" % (t, h)
+        D, TL, Z, ts = F(m, 0, n), F(m, n, 2 * n), F(m, 2 * n, 3 * n), F(m, 3 * n, 4 * n)
+        B = ["p%d" % (4 * h + i) for i in range(4)]
+        ID, N8, BD = F("ID"), F("N8192"), F("BD")
+
+        def bf(i, k=1):
+            return F("bf" + H, i * n, (i + k) * n)
+
+        def f3(a, b):
+            return F("f3" + H, a, b)
+
+        def lf(i):
+            return F("lf" + H, 8 * i, 8 * i + 5)
+
+        def lu(i):
+            return F("lu" + H, 8 * i, 8 * i + 5)
+
+        def eqs(q, k=1):
+            return F("eq" + H, q * n, (q + k) * n)
+        offT, off1, clk = F("offT" + H), F("off1" + H), F("clkw")
+        TS(offT, TL, 2063.0, OP.add)
+        ACT(F("Y" + H), IND(clk, offT), AF.Copy)
+        for j, qs in enumerate(CH):
+            bk = B[j % 2]
+            for i, q in enumerate(qs):
+                o = F(bk, i * n, i * n + n)
+                MM([(o, Rq(q), TL)] + ([(o, F("NI"), D)] if EQ[j] == "s" else []))
+            if EQ[j] == "s":
+                k = len(qs)
+                ACT(F("ea" + H, 0, k * n), F(bk, 0, k * n), AF.Abs)
+                ACT(eqs(qs[0], k), F("ea" + H, 0, k * n), AF.Relu, 1.0, -1.0)
+            else:
+                for i, q in enumerate(qs):
+                    TT(eqs(q), D, F(bk, i * n, i * n + n), OP.is_equal)
+        cdp, ctp = F(B[2], 0, n), F(B[2], n, 2 * n)
+        for j, qs in enumerate(CH):
+            MM([(cdp, F("I4096"), eqs(q)) for q in qs], j < 2, j > 0)
+        for j, qs in enumerate(CH):
+            MM([(ctp, Sq(q), eqs(q)) for q in qs], j < 2, j > 0)
+        d1 = f3(96, 176)
+        TT(d1, D, cdp, OP.subtract)
+        TS(off1, d1, -2048.0, OP.max, 2063.0, OP.add)
+        ACT(F("X" + H), IND(clk, off1), AF.Copy)
+        fl = bf(0)
+        ACT(fl, d1, AF.Sign, 2047.5)
+        cdb, ctb = bf(1), bf(2)
+        ACT(bf(1, 2), F(B[2], 0, 2 * n), AF.Copy, 0.0, 1.0 / 4096)
+        zps, tlp = F(B[3], 400, 480), F(B[3], 320, 400)
+        MM([(zps, ID, Z)])
+        MM([(tlp, ID, TL)])
+        for q in range(16):
+            TT(F("mn" + H, q * n, q * n + n), F("Y" + H, q, G16, 16), zps, OP.min)
+        Gp, scp, kbp = F(B[1], 0, n), F(B[0], 0, n), F(B[0], n, 2 * n)
+        MM([(Gp, BD, Z)] + [(Gp, Sq(q), F("Y" + H, q, G16, 16)) for q in range(16)])
+        for j, qs in enumerate(CH):
+            MM([(scp, Sq(q), F("mn" + H, q * n, q * n + n)) for q in qs], j < 2, j > 0)
+        nk = f3(0, n)
+        ACT(nk, scp, AF.Identity, F("lim"), 2.0)
+        vt, vs, vb = f3(176, 272), f3(272, 368), f3(368, 464)
+        VT(vt, f3(0, 96))
+        SC(vs, F("segV"), vt, -1000000.0, OP.min, OP.max)
+        VT(vb, vs)
+        MM([(kbp, F("R15f"), f3(368, 448))])
+        oh, far, fc, rs = bf(3), bf(4), bf(5), bf(6)
+        TT(far, nk, Gp, OP.is_lt)
+        TT(fc, far, ctp, OP.mult)
+        TT(oh, nk, kbp, OP.is_equal)
+        TT(ts, oh, tlp, OP.mult)
+        ACT(rs, ts, AF.Relu, -2049.0, -1.0)
+        lst = F(B[0], 160, 170)
+        MM([(lst, Sq(r), F(m, 2 * n + r, 4 * n, 16)) for r in range(16)] + [(lst, BD, F("bia"))])
+        cp = F(B[1], n, 2 * n)
+        MM([(cp, BD, fl), (cp, F("BDa"), fc), (cp, F("BDr"), rs)])
+        nm1, sq, q0, nm2, nm3, abm = bf(7), bf(9), bf(10), bf(11), bf(12), bf(18)
+        ACT(sq, cp, AF.Square, 32.5)
+        ACT(q0, cp, AF.Abs, 2048.0, 128.0)
+        ACT(nm1, cp, AF.Relu, -15.0, -1.0)
+        ACT(nm2, cp, AF.Relu, 80.0)
+        if not last:
+            ACT(abm, cp, AF.Relu, -65536.0 * 80, -65536.0)
+            TT(bf(8), cdp, abm, OP.is_gt)
+            ACT(bf(22), bf(8), AF.Copy, 0.0, 1.0, F("ac", h, h + 1))
+        ACT(nm3, sq, AF.Relu, -324.0)
+        sql = F(B[0], 170, 180)
+        MM([(sql, Sq(r), F("bf" + H, 9 * n + r, 11 * n, 16)) for r in range(16)])
+        TS(lu(0), F(B[0], 165, 170), 2064.0, OP.add)
+        yk = bf(13)
+        ACT(yk, IND(clk, lu(0)), AF.Copy)
+        CP(F("li" + H, 0, 10), lst)
+        TS(F("uv" + H), F("li" + H, 0, 10), 255, OP.bitwise_and)
+        uu, v32 = F("uv" + H, 0, 5), F("uv" + H, 5, 10)
+        TT(lf(0), v32, uu, OP.subtract)
+        nu = lf(1)
+        TS(nu, F(B[0], 170, 175), 5184.0, OP.is_gt)
+        TT(F("pv", 5 * h, 5 * h + 5), v32, F(B[0], 175, 180), OP.max)
+        TT(lf(2), lf(0), nu, OP.mult)
+        TT(lf(3), lf(2), uu, OP.add)
+        CP(lu(1), lf(3))
+        cs, csD, csT = F("hf" + H), F("hf" + H, 0, n), F("hf" + H, n, 2 * n)
+        TS(csD, IND(F("sct", 0, 256), lu(1)), -2048.0, OP.add)
+        CP(csT, IND(F("stt"), lu(1)))
+        for j in range(6):
+            bk = B[j % 2]
+            qs = range(3 * j, min(3 * j + 3, 16))
+            for i, q in enumerate(qs):
+                o = F(bk, 160 * i, 160 * i + 160)
+                MM([(o, Rq(q), F(m, 0, 2 * n)), (o, F("NI"), cs)])
+            for i, q in enumerate(qs):
+                ACT(F("ab" + H, q, 2 * G16, 16), F(bk, 160 * i, 160 * i + 160), AF.Abs)
+        for e in range(2):
+            SC(F("sm" + H, e * G16, (e + 1) * G16), F("segM", 0, G16), F("ab" + H, e * G16, (e + 1) * G16), 0.0, OP.max, OP.min)
+        dg, tg, t1p = F(B[2], 160, 240), F(B[2], 240, 320), F(B[3], 320, 400)
+        MM([(dg, ID, D), (dg, N8, cdb), (dg, N8, nm1)])
+        MM([(tg, ID, TL), (tg, F("N25"), ctb), (tg, N8, oh), (tg, N8, nm1)])
+        MM([(t1p, ID, TL), (t1p, F("N25"), ctb), (t1p, N8, oh)])
+        ACT(F("t1s", h * n, h * n + n), t1p, AF.Relu, 2048.0)
+        km, kx = bf(14, 2), f3(464, 624)
+        ACT(km, F(B[2], 160, 320), AF.Relu, 2048.0)
+        TS(f3(464, 544), dg, -2048.0, OP.max)
+        TS(f3(544, 624), tg, -2050.0, OP.max)
+        SC(F("tp" + H), F("seg0"), F("X" + H), 0.0, OP.mult, OP.max)
+        zd, z1, z2, z4 = [F(B[3], i * n, i * n + n) for i in range(4)]
+        MM([(zd, ID, Z), (zd, F("NI"), yk)])
+        A2 = bf(19)
+        ACT(A2, zd, AF.Abs)
+        MM([(z1, F("HI"), yk), (z1, F("HI"), F("tp" + H, 15, G16, 16)), (z1, F("N512"), nm1)])
+        MM([(z2, ID, A2), (z2, F("N512"), nm2)])
+        MM([(z4, ID, Z), (z4, F("N512"), nm3)])
+        ACT(f3(624, 704), z1, AF.Identity, -0.25)
+        TT(f3(704, 784), f3(624, 704), z2, OP.max)
+        TT(f3(784, 864), f3(704, 784), z4, OP.max)
+        o = "out%d%d" % (t, h)
+        zo = F("fin", 320 + h * n, 320 + h * n + n) if last else F(o, 160, 240)
+        TS(zo, f3(784, 864), 8388608.0, OP.add, 8388608.0, OP.subtract)
+        hp, hd = F(B[0], 0, 2 * n), bf(16, 2)
+        for e in range(2):
+            x = F(B[0], e * n, e * n + n)
+            MM([(x, ID, F("sm" + H, e * G16 + 15, (e + 1) * G16, 16)), (x, ID, nm1)])
+        ACT(hd, hp, AF.Relu, 1.0, -1.0)
+        rp = F(B[2], 320, 480)
+        MM([(rp, ID, cs), (rp, N8, km), (rp, N8, hd)])
+        if last:
+            TT(f3(944, 1104), kx, rp, OP.max)
+            TS(F("fin", h * n, h * n + n), f3(944, 1024), 2047.0, OP.add, -1.0, OP.max)
+            TS(F("fin", 160 + h * n, 160 + h * n + n), f3(1024, 1104), 2047.0, OP.add, -1.0, OP.max)
+        else:
+            TT(F(o, 0, 160), kx, rp, OP.max)
+            add("g", "send", (t, h), [F(o)], [], 200)
+            add("n", "arrive", (t, h), [], [F("msg%d%d" % (t + 1, h), 0, 240)], 0, arr=(t + 1, h))
+
+    def proofs(t):
+        pb = "p7"
+        TS(F("pvb"), F("pv"), 4096.0, OP.min)
+        VB, lp, ll = F(pb, 0, NM), F(pb, NM, 2 * NM), F(pb, 488, 498)
+        for r in range(16):
+            MM([(F(pb, r, NM, 16), Rq(r), F("pvb"))])
+        ACT(F("VBs"), VB, AF.Copy)
+        TT(F("VL"), F("VBs"), F("LOW"), OP.max)
+        TT(F("eb"), IND(F("pv"), F("co")), F("VL"), OP.is_equal)
+        lst = [(lp, F("BD"), F("eb"))]
+        a = 0
+        for c in range(1, 10):
+            TS(F("el", a, a + 16 * c), F("VBs", 0, 16 * c), F("pv", c, c + 1), OP.is_equal)
+            lst.append((F(pb, NM, NM + 16 * c), F("BD"), F("el", a, a + 16 * c)))
+            a += 16 * c
+        MM(lst)
+        ACT(F("lo"), lp, AF.Copy)
+        MM([(ll, Sq(r), F("lo", r, NM, 16)) for r in range(16)])
+        TS(F("l0"), ll, 0.5, OP.is_gt, 4096.0, OP.mult)
+        TT(F("xa"), F("l0"), F("pv"), OP.add)
+        TT(F("xa"), F("xa"), F("DUM"), OP.min)
+        CP(F("sou"), F("xa"))
+        CP(IND(F("sct"), F("sou")), F("t1s"))
+
+    def count():
+        pa = F("p7", 504, 505)
+        MM([(pa, F("BDf"), F("ac", 0, 1)), (pa, F("BDf"), F("ac", 1, 2))])
+        TT(F("As"), F("As"), pa, OP.add)
+        TS(F("Am"), F("As"), 31, OP.bitwise_and)
+        TS(F("lim"), F("Am"), 8.0, OP.mult, F("thc"), OP.add)
+
+    for t in range(VIS):
+        for h in range(NH):
+            visit(t, h)
+        if t < VIS - 1:
+            count()
+        proofs(t)
+    TS(F("yso"), F("sct", 0, 256), -1.0, OP.add)
+    add("y", "sto", [("yd", 0), ("yt", 160), ("yz", 320)], [F("fin")], [], 100, dma="wr0", lat=2500)
+    add("y", "stys", None, [F("yso")], [], 50, dma="wr1", lat=2500)
+    return ops
+
+
+def _overlap(a, b):
+    if a[0] != b[0] or a[1] >= b[2] or b[1] >= a[2]:
+        return False
+    return not (a[3] == b[3] and a[3] > 1 and (a[1] - b[1]) % a[3])
+
+
+def _covers(a, b):
+    return a[3] == 1 and a[1] <= b[1] and a[2] >= b[2] or a == b
+
+
+def _deps(ops):
+    hist = {}
+    sends = {}
+    for o in ops:
+        dep = {}
+        acc = [(x, False) for x in o["r"]] + [(x, True) for x in o["w"]]
+        for (x, wr) in acc:
+            psum = _W[x[0]] == "psum"
+            for (y, ywr, yo) in hist.get(x[0], []):
+                if yo is o:
+                    continue
+                same = yo["q"] == o["q"]
+                if psum and not same:
+                    dep[yo["id"]] = True
+                elif psum and o["q"] == "t":
+                    dep.setdefault(yo["id"], False)
+                elif (wr or ywr) and _overlap(x, y):
+                    need = (not same) or (ywr and o["q"] != "t")
+                    dep[yo["id"]] = dep.get(yo["id"], False) or need
+        for (x, wr) in acc:
+            L = hist.setdefault(x[0], [])
+            if wr:
+                ps = _W[x[0]] == "psum"
+                L[:] = [e for e in L if e[2] is o or not (_covers(x, e[0]) and (not ps or e[2]["q"] == o["q"]))]
+            L.append((x, wr, o))
+        if o["call"] == "send":
+            sends[o["args"]] = o["id"]
+        if o["call"] == "arrive":
+            dep[sends[o["args"]]] = False
+        o["dep"] = dep
+
+
+LAT = {"x": 90.0, "own": 55.0, "arr": 3500.0, "fix": 15.0}
+
+
+def _schedule(ops, seed):
+    succ = [[] for _ in ops]
+    for o in ops:
+        for d in o["dep"]:
+            succ[d].append(o["id"])
+
+    def dly(a, b):
+        if a["call"] == "send":
+            return LAT["arr"] if b["call"] == "arrive" else 0.0
+        if "dma" in a:
+            return a["lat"]
+        if not b["dep"][a["id"]]:
+            return 0.0
+        return LAT["own"] if a["q"] == b["q"] else LAT["x"]
+    rng = np.random.default_rng(seed)
+    var = (rng.random(len(ops)) * 600.0 * (seed % 4)).tolist()
+    pri = [0.0] * len(ops)
+    for o in reversed(ops):
+        pri[o["id"]] = o["cost"] + max([pri[s] + dly(o, ops[s]) for s in succ[o["id"]]] + [0.0])
+    pri = [a + b for a, b in zip(pri, var)]
+    left = [len(o["dep"]) for o in ops]
+    rt = [0.0] * len(ops)
+    ready, free, order, start, end = {}, {}, {}, [0.0] * len(ops), 0.0
+    for o in ops:
+        if not left[o["id"]]:
+            ready.setdefault(o["q"], []).append(o["id"])
+    for _ in range(len(ops)):
+        best = None
+        for q, L in ready.items():
+            f = free.get(q, 0.0)
+            for i in L:
+                k = (rt[i] if q == "n" else max(f, rt[i]), -pri[i])
+                if best is None or k < best[0]:
+                    best = (k, q, i)
+        (s, _p), q, i = best
+        ready[q].remove(i)
+        o = ops[i]
+        e = s + o["cost"] + (0.0 if q == "n" else LAT["fix"])
+        start[i] = s
+        free[q] = e
+        end = max(end, e)
+        order.setdefault(q, []).append(i)
+        for x in succ[i]:
+            rt[x] = max(rt[x], e + dly(o, ops[x]))
+            left[x] -= 1
+            if not left[x]:
+                ready.setdefault(ops[x]["q"], []).append(x)
+    return end, seed, order, start
+
+
+_CACHE = {}
+SEMQ = {"v": "sv", "s": "ss", "t": "st_", "g": "sg"}
+
+
+def _plan():
+    if "p" in _CACHE:
+        return _CACHE["p"]
+    ops = _build()
+    _deps(ops)
+    end, _s, order, start = min(_schedule(ops, s) for s in range(SEEDS))
+    cnt = {}
+    for q, L in order.items():
+        for i in L:
+            o = ops[i]
+            o["start"] = start[i]
+            if "dma" in o:
+                o["tok"] = (o["dma"], 48 if o["call"] == "sto" else 16)
+            elif o["call"] == "arrive":
+                o["tok"] = ("arr%d%d" % o["arr"], None)
+            elif o["call"] != "send":
+                cnt[SEMQ[q]] = cnt.get(SEMQ[q], 0) + 1
+                o["tok"] = (SEMQ[q], cnt[SEMQ[q]])
+    known = {}
+    for i in sorted((i for L in order.values() for i in L), key=lambda i: (ops[i]["start"], i)):
+        o = ops[i]
+        kn = known.setdefault(o["q"], {})
+        w = {}
+        for d in sorted((d for d, nd in o["dep"].items() if nd), key=lambda d: -ops[d]["start"]):
+            s, v = ops[d]["tok"]
+            if v is None:
+                v = 1
+            if kn.get(s, 0) >= v:
+                continue
+            w[s] = max(w.get(s, 0), v)
+            for s2, v2 in list(ops[d]["kn"].items()) + [(s, v)]:
+                kn[s2] = max(kn.get(s2, 0), v2)
+        o["wait"] = sorted(w.items())
+        o["kn"] = dict(kn)
+    _CACHE["p"] = (ops, order, cnt, end)
+    return _CACHE["p"]
+
+
+def rank_program(g, core, T, topo):
+    rank = T.rank_of(core)
+    if rank is None:
+        return
+    ops, order, cnt, _end = _plan()
+    hops = [1, 4, 2]
+    eng = {"v": g.vector, "s": g.scalar, "t": g.tensor, "g": g, "y": g.sync}
+    N = len(T.cores)
+    arrn = [0] + [len(topo.engines(T.cores[(rank - hops[t]) % N], core)) for t in range(VIS - 1)]
+
+    def ap(x):
+        if not isinstance(x, tuple):
+            return x
+        if x[0] == "IND":
+            return ap(x[1]).indirect(ap(x[2]))
+        if x[3] == 1:
+            return T[x[0]][:, x[1]:x[2]]
+        return T[x[0]][:, x[1]:x[2]:x[3]]
+
+    nsend = 0
+    for q in ("y", "s", "v", "t", "g"):
+        e = eng[q]
+        for i in order[q]:
+            o = ops[i]
+            for s, v in o["wait"]:
+                e.wait_ge(T.sem[s], arrn[int(s[3])] if s[:3] == "arr" else v)
+            a, call = o["args"], o["call"]
+            if call == "send":
+                t, h = a
+                dst = T.cores[(rank + hops[t]) % N]
+                rid, pid = topo.addr(dst, core)
+                g.remote_dma(T["msg%d%d" % (t + 1, h)][:, 0:240], T["out%d%d" % (t, h)][:], T.sem["arr%d%d" % (t + 1, h)], T.sem.snd, pid, rid, topo.mask(core, dst))
+                nsend += len(topo.engines(core, dst))
+                continue
+            if call == "ld":
+                e.dma_start(ap(a[0]), T[a[1]][:, :]).then_inc(T.sem[o["dma"]], 16)
+                continue
+            if call == "sto":
+                for nm, c in a:
+                    e.dma_start(T[nm][:, :], T.fin[:, c:c + NM]).then_inc(T.sem[o["dma"]], 16)
+                continue
+            if call == "stys":
+                e.dma_start(T.ys[:, :], T.yso[:, :]).then_inc(T.sem[o["dma"]], 16)
+                continue
+            if call == "mm":
+                lst, st, sp = a
+                for k, (oo, l, r) in enumerate(lst):
+                    ins = e.matmul(ap(oo), ap(l), ap(r), st and k == 0, sp and k == len(lst) - 1)
+            elif call == "tt":
+                ins = e.tensor_tensor(ap(a[0]), ap(a[1]), ap(a[2]), a[3])
+            elif call == "ts":
+                if a[5] is None:
+                    ins = e.tensor_scalar(ap(a[0]), ap(a[1]), ap(a[2]), None, a[4])
+                else:
+                    ins = e.tensor_scalar(ap(a[0]), ap(a[1]), ap(a[2]), ap(a[3]), a[4], a[5])
+            elif call == "cp":
+                ins = e.tensor_copy(ap(a[0]), ap(a[1]))
+            elif call == "ms":
+                ins = e.memset(ap(a[0]), a[1])
+            elif call == "sc":
+                ins = e.tensor_tensor_scan(ap(a[0]), ap(a[1]), ap(a[2]), a[3], a[4], a[5])
+            elif call == "vt":
+                ins = e.transpose(ap(a[0]), ap(a[1]))
+            elif call == "act":
+                kw = {} if a[5] is None else {"accum_out": ap(a[5])}
+                ins = e.activation(ap(a[0]), ap(a[1]), a[2], ap(a[3]), ap(a[4]), **kw)
+            elif call == "iota":
+                ins = e.iota(ap(a[0]), a[1], a[2], a[3])
+            ins.then_inc(T.sem[o["tok"][0]], 1)
+    g.wait_ge(T.sem.snd, nsend)
+    for s, v in sorted(cnt.items()):
+        g.wait_ge(T.sem[s], v)
+    g.wait_ge(T.sem.wr0, 48)
+    g.wait_ge(T.sem.wr1, 16)

@@ -1,4 +1,3 @@
-import numpy as np
 from concourse.mybir import AluOpType, ActivationFunctionType
 
 OP = AluOpType
@@ -10,7 +9,11 @@ G16 = 16 * n
 VIS = 4
 CW = 4112
 EQ = "vvs"
-SEEDS = 24
+PH = ["S", 0, 0]
+BIAS = {('y', 1): -6593, ('P', 0): -437, ('m', 0): -1080, ('l', 1): 1848, (3, 1): -469, ('l', 0): -1593, ('A', 0): -7776, ('m', 1): -1226, (0, 0): -1353,
+        ('c', 0): 1837, ('k', 1): 116, ('z', 0): 2276, (2, 1): 1600, (2, 0): -144, ('h', 1): 702, ('d', 1): 926, ('q', 1): -665, ('z', 1): -13,
+        ('r', 0): 25389, (1, 1): -21, ('d', 0): 380, ('h', 0): -302, ('r', 1): -434, ('c', 1): -2889, (3, 0): -495, (1, 0): -675, ('y', 0): -6007,
+        ('S', 0): -356, ('q', 0): -98, ('k', 0): 13095, (0, 1): -341, ('x', 0): -1682, ('x', 1): 84}
 
 SCRATCH = {}
 _W = {}
@@ -27,7 +30,7 @@ _buf("clkw", CW, "bfloat16")
 for _nm, _c in (("dli", NM), ("tli", NM), ("sci", 256), ("sti", 256), ("thi", 1)):
     _buf(_nm, _c, "int32")
 _buf("zin", NM, "bfloat16")
-_buf("tf", 256, "float32")
+_buf("tf", 256, "float32"); _buf("tf2", 256, "float32")
 _buf("sct", 256 + NM, "float32")
 _buf("stt", 256, "float32")
 _buf("ic", NM, "int32"); _buf("ik", 1, "int32"); _buf("id4", NM, "int32"); _buf("im", NM, "int32")
@@ -36,7 +39,7 @@ for _nm in ("BD", "ID", "I4096", "N25", "NI", "HI", "N512", "N8192", "BDa", "BDr
     _buf(_nm, 128, "bfloat16")
 _buf("BDf", 128, "float32"); _buf("R15f", 128, "float32")
 _buf("RR", 2048, "float16"); _buf("SS", 2048, "bfloat16"); _buf("bia", 10, "bfloat16")
-_buf("seg0", G16, "bfloat16"); _buf("segM", 2 * G16, "bfloat16"); _buf("segV", 96, "float32")
+_buf("seg0", G16, "bfloat16"); _buf("segM", G16, "bfloat16"); _buf("segV", 96, "float32")
 _buf("LOW", NM, "bfloat16"); _buf("co", 10, "uint16"); _buf("DUM", 10, "float32"); _buf("dmi", 10, "int32")
 _buf("thc", 1, "float32"); _buf("lim", 1, "float32"); _buf("As", 1, "int32"); _buf("Am", 1, "int32"); _buf("ac", 2, "float32")
 _buf("t1s", NM, "float32"); _buf("pv", 10, "float32"); _buf("pvb", 10, "bfloat16")
@@ -71,7 +74,7 @@ def _build():
     ops = []
 
     def add(q, call, args, reads, writes, cost, **kw):
-        d = {"q": q, "call": call, "args": args, "r": reads, "w": writes, "cost": cost, "id": len(ops)}
+        d = {"ph": tuple(PH), "q": q, "call": call, "args": args, "r": reads, "w": writes, "cost": cost, "id": len(ops)}
         d.update(kw)
         ops.append(d)
 
@@ -139,6 +142,12 @@ def _build():
     def LD(q, out, name, sem):
         add(q, "ld", (out, name), [], [out], 50, dma=sem, lat=6000 if name == "clk" else 2500)
 
+    def IO(x, c):
+        add("g", "iota", (x, [[0, wid(x)]], c, 0), [], [x], 130 + 1.7 * wid(x))
+
+    def AS(x, c):
+        add("g", "asel", (x, [[0, wid(x) // 16], [1, 16]], c), [x], [x], 170 + 1.7 * wid(x))
+
     LD("y", F("tli"), "tl", "ld0")
     LD("y", F("dli"), "dl", "ld1")
     LD("y", F("zin"), "z0", "ld2")
@@ -161,25 +170,25 @@ def _build():
     TS(F("ID"), F("ic", 0, 128), F("kf", 0, 1), OP.is_equal)
     for q in range(16):
         TS(F("RR", 128 * q, 128 * q + 128), F("BD"), F("K16", q, q + 1), OP.mult)
-    MS(F("SS"), 0.0)
+    IO(F("SS"), 0)
+    IO(F("segM"), 0)
+    AS(F("segM"), 8192.0)
+    IO(F("seg0"), 1)
+    AS(F("seg0"), 0.0)
     for q in range(16):
         ACT(F("SS", 129 * q, 128 * q + 128, 16), F("BD", q, 128, 16), AF.Copy)
     for nm, src, c in (("I4096", "ID", 4096.0), ("NI", "ID", -1.0), ("HI", "ID", 0.5), ("N512", "ID", -512.0), ("N8192", "ID", -8192.0),
-                       ("N25", "ID", -33554432.0), ("BDa", "BD", -128.0), ("BDr", "BD", -34.0), ("BDf", "BD", 1.0)):
+                       ("N25", "ID", -33554432.0), ("BDa", "BD", -128.0), ("BDr", "BD", -2.125), ("BDf", "BD", 1.0)):
         ACT(F(nm), F(src), AF.Copy, 0.0, c)
     ACT(F("R15f"), F("BD"), AF.Copy, 0.0, F("K16", 15, 16))
     MS(F("segV"), 1000000.0)
     MS(F("segV", 0, 96, 16), -1000000.0)
-    MS(F("seg0"), 1.0)
-    MS(F("seg0", 0, G16, 16), 0.0)
-    MS(F("segM"), 0.0)
-    MS(F("segM", 0, 2 * G16, 16), 8192.0)
     MS(F("bia"), 0.0)
     MS(F("bia", 5, 10), -1.0 / 16)
     for h in range(NH):
         MS(F("f3%d" % h, 0, 96), 0.0)
     CP(F("tf", 0, NM), F("tli"))
-    TS(F("t1s"), F("tf", 0, NM), 3.0, OP.mult)
+    ACT(F("t1s"), F("tf", 0, NM), AF.Copy, 0.0, 3.0)
     TT(F("t1s"), F("t1s"), F("tf", 0, NM), OP.min)
     for h in range(NH):
         m = "msg0%d" % h
@@ -193,10 +202,10 @@ def _build():
     MS(F("As"), 0)
     TS(F("sct", 0, 256), F("sci"), 1.0, OP.add)
     MS(F("sct", 256, 256 + NM), 0.0)
-    CP(F("tf"), F("sti"))
-    TS(F("stt"), F("tf"), 3.0, OP.mult)
-    TT(F("stt"), F("stt"), F("tf"), OP.min)
-    TS(F("stt"), F("stt"), -2047.0, OP.add)
+    CP(F("tf2"), F("sti"))
+    ACT(F("stt"), F("tf2"), AF.Copy, 0.0, 3.0)
+    TT(F("stt"), F("stt"), F("tf2"), OP.min)
+    ACT(F("stt"), F("stt"), AF.Copy, -2047.0)
     TS(F("im"), F("ic"), 15, OP.bitwise_and)
     TS(F("LOW"), F("im"), F("kf", 2, 3), OP.is_ge, 1024.0, OP.mult)
     CP(F("co"), F("ic", 0, 10))
@@ -233,8 +242,10 @@ def _build():
         def eqs(q, k=1):
             return F("eq" + H, q * n, (q + k) * n)
         offT, off1, clk = F("offT" + H), F("off1" + H), F("clkw")
+        PH[0] = "y"
         TS(offT, TL, 2063.0, OP.add)
         ACT(F("Y" + H), IND(clk, offT), AF.Copy)
+        PH[0] = "q"
         for j, qs in enumerate(CH):
             bk = B[j % 2]
             for i, q in enumerate(qs):
@@ -248,10 +259,15 @@ def _build():
                 for i, q in enumerate(qs):
                     TT(eqs(q), D, F(bk, i * n, i * n + n), OP.is_equal)
         cdp, ctp = F(B[2], 0, n), F(B[2], n, 2 * n)
+        ACT(bf(21), TL, AF.Sign, 2048.5)
+        MM([(F(B[3], 240, 320), BD, bf(21))])
+        rs = bf(6)
+        ACT(rs, F(B[3], 240, 320), AF.Relu, -15.0, -1.0)
         for j, qs in enumerate(CH):
             MM([(cdp, F("I4096"), eqs(q)) for q in qs], j < 2, j > 0)
         for j, qs in enumerate(CH):
             MM([(ctp, Sq(q), eqs(q)) for q in qs], j < 2, j > 0)
+        PH[0] = "x"
         d1 = f3(96, 176)
         TT(d1, D, cdp, OP.subtract)
         TS(off1, d1, -2048.0, OP.max, 2063.0, OP.add)
@@ -260,6 +276,7 @@ def _build():
         ACT(fl, d1, AF.Sign, 2047.5)
         cdb, ctb = bf(1), bf(2)
         ACT(bf(1, 2), F(B[2], 0, 2 * n), AF.Copy, 0.0, 1.0 / 4096)
+        PH[0] = "m"
         zps, tlp = F(B[3], 400, 480), F(B[3], 320, 400)
         MM([(zps, ID, Z)])
         MM([(tlp, ID, TL)])
@@ -269,6 +286,7 @@ def _build():
         MM([(Gp, BD, Z)] + [(Gp, Sq(q), F("Y" + H, q, G16, 16)) for q in range(16)])
         for j, qs in enumerate(CH):
             MM([(scp, Sq(q), F("mn" + H, q * n, q * n + n)) for q in qs], j < 2, j > 0)
+        PH[0] = "k"
         nk = f3(0, n)
         ACT(nk, scp, AF.Identity, F("lim"), 2.0)
         vt, vs, vb = f3(176, 272), f3(272, 368), f3(368, 464)
@@ -276,14 +294,14 @@ def _build():
         SC(vs, F("segV"), vt, -1000000.0, OP.min, OP.max)
         VT(vb, vs)
         MM([(kbp, F("R15f"), f3(368, 448))])
-        oh, far, fc, rs = bf(3), bf(4), bf(5), bf(6)
+        oh, far, fc = bf(3), bf(4), bf(5)
         TT(far, nk, Gp, OP.is_lt)
         TT(fc, far, ctp, OP.mult)
         TT(oh, nk, kbp, OP.is_equal)
         TT(ts, oh, tlp, OP.mult)
-        ACT(rs, ts, AF.Relu, -2049.0, -1.0)
         lst = F(B[0], 160, 170)
         MM([(lst, Sq(r), F(m, 2 * n + r, 4 * n, 16)) for r in range(16)] + [(lst, BD, F("bia"))])
+        PH[0] = "c"
         cp = F(B[1], n, 2 * n)
         MM([(cp, BD, fl), (cp, F("BDa"), fc), (cp, F("BDr"), rs)])
         nm1, sq, q0, nm2, nm3, abm = bf(7), bf(9), bf(10), bf(11), bf(12), bf(18)
@@ -296,6 +314,7 @@ def _build():
             TT(bf(8), cdp, abm, OP.is_gt)
             ACT(bf(22), bf(8), AF.Copy, 0.0, 1.0, F("ac", h, h + 1))
         ACT(nm3, sq, AF.Relu, -324.0)
+        PH[0] = "l"
         sql = F(B[0], 170, 180)
         MM([(sql, Sq(r), F("bf" + H, 9 * n + r, 11 * n, 16)) for r in range(16)])
         TS(lu(0), F(B[0], 165, 170), 2064.0, OP.add)
@@ -314,16 +333,17 @@ def _build():
         cs, csD, csT = F("hf" + H), F("hf" + H, 0, n), F("hf" + H, n, 2 * n)
         TS(csD, IND(F("sct", 0, 256), lu(1)), -2048.0, OP.add)
         CP(csT, IND(F("stt"), lu(1)))
-        for j in range(6):
-            bk = B[j % 2]
-            qs = range(3 * j, min(3 * j + 3, 16))
-            for i, q in enumerate(qs):
-                o = F(bk, 160 * i, 160 * i + 160)
-                MM([(o, Rq(q), F(m, 0, 2 * n)), (o, F("NI"), cs)])
-            for i, q in enumerate(qs):
-                ACT(F("ab" + H, q, 2 * G16, 16), F(bk, 160 * i, 160 * i + 160), AF.Abs)
+        PH[0] = "h"
         for e in range(2):
+            for j, qs in enumerate(CH):
+                bk = B[(j + e) % 2]
+                for i, q in enumerate(qs):
+                    o = F(bk, i * n, i * n + n)
+                    MM([(o, Rq(q), F(m, e * n, e * n + n)), (o, F("NI"), F("hf" + H, e * n, e * n + n))])
+                for i, q in enumerate(qs):
+                    ACT(F("ab" + H, e * G16 + q, (e + 1) * G16, 16), F(bk, i * n, i * n + n), AF.Abs)
             SC(F("sm" + H, e * G16, (e + 1) * G16), F("segM", 0, G16), F("ab" + H, e * G16, (e + 1) * G16), 0.0, OP.max, OP.min)
+        PH[0] = "d"
         dg, tg, t1p = F(B[2], 160, 240), F(B[2], 240, 320), F(B[3], 320, 400)
         MM([(dg, ID, D), (dg, N8, cdb), (dg, N8, nm1)])
         MM([(tg, ID, TL), (tg, F("N25"), ctb), (tg, N8, oh), (tg, N8, nm1)])
@@ -333,6 +353,7 @@ def _build():
         ACT(km, F(B[2], 160, 320), AF.Relu, 2048.0)
         TS(f3(464, 544), dg, -2048.0, OP.max)
         TS(f3(544, 624), tg, -2050.0, OP.max)
+        PH[0] = "z"
         SC(F("tp" + H), F("seg0"), F("X" + H), 0.0, OP.mult, OP.max)
         zd, z1, z2, z4 = [F(B[3], i * n, i * n + n) for i in range(4)]
         MM([(zd, ID, Z), (zd, F("NI"), yk)])
@@ -347,6 +368,7 @@ def _build():
         o = "out%d%d" % (t, h)
         zo = F("fin", 320 + h * n, 320 + h * n + n) if last else F(o, 160, 240)
         TS(zo, f3(784, 864), 8388608.0, OP.add, 8388608.0, OP.subtract)
+        PH[0] = "r"
         hp, hd = F(B[0], 0, 2 * n), bf(16, 2)
         for e in range(2):
             x = F(B[0], e * n, e * n + n)
@@ -396,10 +418,14 @@ def _build():
 
     for t in range(VIS):
         for h in range(NH):
+            PH[1:] = [t, h]
             visit(t, h)
+        PH[:] = ["A", t, 0]
         if t < VIS - 1:
             count()
+        PH[:] = ["P", t, 0]
         proofs(t)
+    PH[:] = ["E", 0, 0]
     TS(F("yso"), F("sct", 0, 256), -1.0, OP.add)
     add("y", "sto", [("yd", 0), ("yt", 160), ("yz", 320)], [F("fin")], [], 100, dma="wr0", lat=2500)
     add("y", "stys", None, [F("yso")], [], 50, dma="wr1", lat=2500)
@@ -448,10 +474,11 @@ def _deps(ops):
         o["dep"] = dep
 
 
-LAT = {"x": 90.0, "own": 55.0, "arr": 3500.0, "fix": 15.0}
+LAT = {"x": 130.0, "own": 80.0, "arr": 3800.0, "fix": 20.0}
+SCALE = 1.1
 
 
-def _schedule(ops, seed):
+def _schedule(ops, seed=0):
     succ = [[] for _ in ops]
     for o in ops:
         for d in o["dep"]:
@@ -465,12 +492,10 @@ def _schedule(ops, seed):
         if not b["dep"][a["id"]]:
             return 0.0
         return LAT["own"] if a["q"] == b["q"] else LAT["x"]
-    rng = np.random.default_rng(seed)
-    var = (rng.random(len(ops)) * 600.0 * (seed % 4)).tolist()
     pri = [0.0] * len(ops)
     for o in reversed(ops):
         pri[o["id"]] = o["cost"] + max([pri[s] + dly(o, ops[s]) for s in succ[o["id"]]] + [0.0])
-    pri = [a + b for a, b in zip(pri, var)]
+    pri = [p + BIAS.get((o["ph"][0], o["ph"][2]), 0.0) + BIAS.get(o["ph"][1:], 0.0) for p, o in zip(pri, ops)]
     left = [len(o["dep"]) for o in ops]
     rt = [0.0] * len(ops)
     ready, free, order, start, end = {}, {}, {}, [0.0] * len(ops), 0.0
@@ -510,7 +535,9 @@ def _plan():
         return _CACHE["p"]
     ops = _build()
     _deps(ops)
-    end, _s, order, start = min(_schedule(ops, s) for s in range(SEEDS))
+    for o in ops:
+        o["cost"] *= SCALE
+    end, _s, order, start = _schedule(ops)
     cnt = {}
     for q, L in order.items():
         for i in L:
@@ -610,7 +637,9 @@ def rank_program(g, core, T, topo):
                 kw = {} if a[5] is None else {"accum_out": ap(a[5])}
                 ins = e.activation(ap(a[0]), ap(a[1]), a[2], ap(a[3]), ap(a[4]), **kw)
             elif call == "iota":
-                ins = e.iota(ap(a[0]), a[1], a[2], a[3])
+                ins = e.iota(ap(a[0]), a[1], a[2], a[3], allow_small_or_imprecise_dtypes=True)
+            elif call == "asel":
+                ins = e.affine_select(ap(a[0]), ap(a[0]), a[1], OP.not_equal, a[2], 0, 0)
             ins.then_inc(T.sem[o["tok"][0]], 1)
     g.wait_ge(T.sem.snd, nsend)
     for s, v in sorted(cnt.items()):

from concourse.mybir import AluOpType, ActivationFunctionType

OP = AluOpType
AF = ActivationFunctionType
NH = 2
n = 80
NM = 160
G16 = 16 * n
VIS = 4
CW = 4112
EQ = "vvs"
PH = ["S", 0, 0]
BIAS = {('y', 1): -6593, ('P', 0): -437, ('m', 0): -1080, ('l', 1): 1848, (3, 1): -469, ('l', 0): -1593, ('A', 0): -7776, ('m', 1): -1226, (0, 0): -1353,
        ('c', 0): 1837, ('k', 1): 116, ('z', 0): 2276, (2, 1): 1600, (2, 0): -144, ('h', 1): 702, ('d', 1): 926, ('q', 1): -665, ('z', 1): -13,
        ('r', 0): 25389, (1, 1): -21, ('d', 0): 380, ('h', 0): -302, ('r', 1): -434, ('c', 1): -2889, (3, 0): -495, (1, 0): -675, ('y', 0): -6007,
        ('S', 0): -356, ('q', 0): -98, ('k', 0): 13095, (0, 1): -341, ('x', 0): -1682, ('x', 1): 84}

SCRATCH = {}
_W = {}


def _buf(name, cols, dtype, where="sbuf"):
    SCRATCH[name] = (where, [128, cols], dtype)
    _W[name] = where


for _i in range(8):
    _buf("p%d" % _i, 512, "float32", "psum")
_buf("clkw", CW, "bfloat16")
for _nm, _c in (("dli", NM), ("tli", NM), ("sci", 256), ("sti", 256), ("thi", 1)):
    _buf(_nm, _c, "int32")
_buf("zin", NM, "bfloat16")
_buf("tf", 256, "float32"); _buf("tf2", 256, "float32")
_buf("sct", 256 + NM, "float32")
_buf("stt", 256, "float32")
_buf("ic", NM, "int32"); _buf("ik", 1, "int32"); _buf("id4", NM, "int32"); _buf("im", NM, "int32")
_buf("kf", 4, "float32"); _buf("kdi", 1, "int32"); _buf("kmi", 1, "int32"); _buf("K16", 16, "float32")
for _nm in ("BD", "ID", "I4096", "N25", "NI", "HI", "N512", "N8192", "BDa", "BDr"):
    _buf(_nm, 128, "bfloat16")
_buf("BDf", 128, "float32"); _buf("R15f", 128, "float32")
_buf("RR", 2048, "float16"); _buf("SS", 2048, "bfloat16"); _buf("bia", 10, "bfloat16")
_buf("seg0", G16, "bfloat16"); _buf("segM", G16, "bfloat16"); _buf("segV", 96, "float32")
_buf("LOW", NM, "bfloat16"); _buf("co", 10, "uint16"); _buf("DUM", 10, "float32"); _buf("dmi", 10, "int32")
_buf("thc", 1, "float32"); _buf("lim", 1, "float32"); _buf("As", 1, "int32"); _buf("Am", 1, "int32"); _buf("ac", 2, "float32")
_buf("t1s", NM, "float32"); _buf("pv", 10, "float32"); _buf("pvb", 10, "bfloat16")
_buf("VBs", NM, "bfloat16"); _buf("VL", NM, "bfloat16"); _buf("eb", NM, "bfloat16"); _buf("el", 16 * 45, "bfloat16")
_buf("lo", NM, "bfloat16"); _buf("l0", 10, "float32"); _buf("xa", 10, "float32"); _buf("sou", 10, "uint16")
_buf("yso", 256, "float32"); _buf("fin", 480, "float32")
for _h in range(NH):
    for _t in range(VIS):
        _buf("msg%d%d" % (_t, _h), 320, "float16")
        if _t < VIS - 1:
            _buf("out%d%d" % (_t, _h), 240, "float16")
    for _nm, _c, _d in (("offT", n, "uint16"), ("off1", n, "uint16"), ("Y", G16, "bfloat16"), ("X", G16, "bfloat16"), ("mn", G16, "bfloat16"),
                        ("eq", G16, "bfloat16"), ("ea", 480, "bfloat16"), ("ab", 2 * G16, "bfloat16"), ("sm", 2 * G16, "bfloat16"),
                        ("tp", G16, "bfloat16"), ("bf", 1840, "bfloat16"), ("f3", 1104, "float32"), ("hf", 160, "float16"),
                        ("li", 16, "int32"), ("uv", 10, "int32"), ("lu", 16, "uint16"), ("lf", 40, "float32")):
        _buf(_nm + str(_h), _c, _d)

SEMAPHORES = ["sv", "ss", "st_", "sg", "snd"] + ["ld%d" % i for i in range(7)] + ["arr%d%d" % (t, h) for t in range(1, VIS) for h in range(NH)] + ["wr0", "wr1"]


def F(name, a=0, b=None, s=1):
    if b is None:
        b = SCRATCH[name][1][1]
    return (name, a, b, s)


def IND(win, off):
    return ("IND", win, off)


def _build():
    ops = []

    def add(q, call, args, reads, writes, cost, **kw):
        d = {"ph": tuple(PH), "q": q, "call": call, "args": args, "r": reads, "w": writes, "cost": cost, "id": len(ops)}
        d.update(kw)
        ops.append(d)

    def rd(*refs):
        res = []
        for x in refs:
            res += [x[1], x[2]] if x[0] == "IND" else [x]
        return res

    def wid(x):
        return 16 * (x[2][2] - x[2][1]) if x[0] == "IND" else -(-(x[2] - x[1]) // x[3])

    def two(x):
        return SCRATCH[x[0]][2] in ("bfloat16", "float16", "uint16")

    def ps(x):
        return _W[x[0]] == "psum"

    CY = 0.83

    def vcost(out, ins, tt):
        k = wid(out)
        if any(x[0] == "IND" for x in ins):
            return 50 + 1.56 * CY * k
        if out[0] == "IND":
            return 50 + 3.8 * CY * k
        if tt:
            k = k if any(ps(x) for x in ins) else 2 * k
        elif all(two(x) for x in ins + [out]):
            k = k / 2
        return max(64, k) * CY

    def TT(out, a, b, op):
        add("v", "tt", (out, a, b, op), rd(a, b), [out], vcost(out, [a, b], True))

    def TS(out, a, s1, op0, s2=None, op1=None):
        sr = [x for x in (s1, s2) if isinstance(x, tuple)]
        add("v", "ts", (out, a, s1, s2, op0, op1), rd(a) + sr, [out], vcost(out, [a], False))

    def CP(out, a):
        w = [out[1]] if out[0] == "IND" else [out]
        add("v", "cp", (out, a), rd(a) + ([out[2]] if out[0] == "IND" else []), w, vcost(out, [a], False))

    def MS(out, c):
        add("v", "ms", (out, c), [], [out], max(64, wid(out) * (0.5 if two(out) else 1)) * CY)

    def SC(out, d0, d1, init, op0, op1):
        add("v", "sc", (out, d0, d1, init, op0, op1), [d0, d1], [out], vcost(out, [d0, d1], False))

    def VT(out, a):
        add("v", "vt", (out, a), [a], [out], vcost(out, [a], False))

    def ACT(out, a, f, bias=0.0, scale=1.0, acc=None):
        k = wid(out)
        c = 65 + 1.56 * CY * k if a[0] == "IND" else max(64, k) * CY
        add("s", "act", (out, a, f, bias, scale, acc), rd(a) + [x for x in (bias, scale) if isinstance(x, tuple)], [out] + ([acc] if acc else []), c)

    def MM(lst, more=False, cont=False):
        c = 0
        for (o, l, r) in lst:
            c += max(64, wid(r)) * 0.42 * (4 if SCRATCH[r[0]][2] == "float32" else 1)
        reads = [x[1] for x in lst] + [x[2] for x in lst]
        add("t", "mm", (lst, not cont, not more), reads, [x[0] for x in lst], c)

    def LD(q, out, name, sem):
        add(q, "ld", (out, name), [], [out], 50, dma=sem, lat=6000 if name == "clk" else 2500)

    def IO(x, c):
        add("g", "iota", (x, [[0, wid(x)]], c, 0), [], [x], 130 + 1.7 * wid(x))

    def AS(x, c):
        add("g", "asel", (x, [[0, wid(x) // 16], [1, 16]], c), [x], [x], 170 + 1.7 * wid(x))

    LD("y", F("tli"), "tl", "ld0")
    LD("y", F("dli"), "dl", "ld1")
    LD("y", F("zin"), "z0", "ld2")
    LD("y", F("thi"), "th", "ld3")
    LD("y", F("sci"), "sc", "ld4")
    LD("y", F("sti"), "st", "ld5")
    LD("s", F("clkw", 16, CW), "clk", "ld6")
    add("g", "iota", (F("ik"), [[0, 1]], 0, 1), [], [F("ik")], 135)
    add("g", "iota", (F("ic"), [[1, NM]], 0, 0), [], [F("ic")], 400)
    add("g", "iota", (F("dmi"), [[16, 10]], 256, 0), [], [F("dmi")], 150)
    MS(F("clkw", 0, 16), -1.0)
    TS(F("kdi"), F("ik"), 4, OP.arith_shift_right)
    TS(F("kmi"), F("ik"), 15, OP.bitwise_and)
    CP(F("kf", 0, 1), F("ik"))
    CP(F("kf", 1, 2), F("kdi"))
    CP(F("kf", 2, 3), F("kmi"))
    TS(F("id4"), F("ic"), 4, OP.arith_shift_right)
    TS(F("BD"), F("id4", 0, 128), F("kf", 1, 2), OP.is_equal)
    TS(F("K16"), F("ic", 0, 16), F("kf", 2, 3), OP.is_equal)
    TS(F("ID"), F("ic", 0, 128), F("kf", 0, 1), OP.is_equal)
    for q in range(16):
        TS(F("RR", 128 * q, 128 * q + 128), F("BD"), F("K16", q, q + 1), OP.mult)
    IO(F("SS"), 0)
    IO(F("segM"), 0)
    AS(F("segM"), 8192.0)
    IO(F("seg0"), 1)
    AS(F("seg0"), 0.0)
    for q in range(16):
        ACT(F("SS", 129 * q, 128 * q + 128, 16), F("BD", q, 128, 16), AF.Copy)
    for nm, src, c in (("I4096", "ID", 4096.0), ("NI", "ID", -1.0), ("HI", "ID", 0.5), ("N512", "ID", -512.0), ("N8192", "ID", -8192.0),
                       ("N25", "ID", -33554432.0), ("BDa", "BD", -128.0), ("BDr", "BD", -2.125), ("BDf", "BD", 1.0)):
        ACT(F(nm), F(src), AF.Copy, 0.0, c)
    ACT(F("R15f"), F("BD"), AF.Copy, 0.0, F("K16", 15, 16))
    MS(F("segV"), 1000000.0)
    MS(F("segV", 0, 96, 16), -1000000.0)
    MS(F("bia"), 0.0)
    MS(F("bia", 5, 10), -1.0 / 16)
    for h in range(NH):
        MS(F("f3%d" % h, 0, 96), 0.0)
    CP(F("tf", 0, NM), F("tli"))
    ACT(F("t1s"), F("tf", 0, NM), AF.Copy, 0.0, 3.0)
    TT(F("t1s"), F("t1s"), F("tf", 0, NM), OP.min)
    for h in range(NH):
        m = "msg0%d" % h
        TS(F(m, n, 2 * n), F("t1s", h * n, h * n + n), -2047.0, OP.add)
        TS(F(m, 0, n), F("dli", h * n, h * n + n), -2047.0, OP.add)
        CP(F(m, 2 * n, 3 * n), F("zin", h * n, h * n + n))
    CP(F("thc"), F("thi"))
    TS(F("kf", 3, 4), F("kf", 2, 3), -1.0 / 16, OP.mult, 31.0 / 32, OP.add)
    TT(F("thc"), F("thc"), F("kf", 3, 4), OP.add)
    CP(F("lim"), F("thc"))
    MS(F("As"), 0)
    TS(F("sct", 0, 256), F("sci"), 1.0, OP.add)
    MS(F("sct", 256, 256 + NM), 0.0)
    CP(F("tf2"), F("sti"))
    ACT(F("stt"), F("tf2"), AF.Copy, 0.0, 3.0)
    TT(F("stt"), F("stt"), F("tf2"), OP.min)
    ACT(F("stt"), F("stt"), AF.Copy, -2047.0)
    TS(F("im"), F("ic"), 15, OP.bitwise_and)
    TS(F("LOW"), F("im"), F("kf", 2, 3), OP.is_ge, 1024.0, OP.mult)
    CP(F("co"), F("ic", 0, 10))
    TS(F("DUM"), F("dmi"), F("kf", 2, 3), OP.add)

    def Rq(q):
        return F("RR", 128 * q, 128 * q + 128)

    def Sq(q):
        return F("SS", 128 * q, 128 * q + 128)

    CH = [list(range(0, 6)), list(range(6, 12)), list(range(12, 16))]

    def visit(t, h):
        last = t == VIS - 1
        H = str(h)
        m = "msg%d%d" % (t, h)
        D, TL, Z, ts = F(m, 0, n), F(m, n, 2 * n), F(m, 2 * n, 3 * n), F(m, 3 * n, 4 * n)
        B = ["p%d" % (4 * h + i) for i in range(4)]
        ID, N8, BD = F("ID"), F("N8192"), F("BD")

        def bf(i, k=1):
            return F("bf" + H, i * n, (i + k) * n)

        def f3(a, b):
            return F("f3" + H, a, b)

        def lf(i):
            return F("lf" + H, 8 * i, 8 * i + 5)

        def lu(i):
            return F("lu" + H, 8 * i, 8 * i + 5)

        def eqs(q, k=1):
            return F("eq" + H, q * n, (q + k) * n)
        offT, off1, clk = F("offT" + H), F("off1" + H), F("clkw")
        PH[0] = "y"
        TS(offT, TL, 2063.0, OP.add)
        ACT(F("Y" + H), IND(clk, offT), AF.Copy)
        PH[0] = "q"
        for j, qs in enumerate(CH):
            bk = B[j % 2]
            for i, q in enumerate(qs):
                o = F(bk, i * n, i * n + n)
                MM([(o, Rq(q), TL)] + ([(o, F("NI"), D)] if EQ[j] == "s" else []))
            if EQ[j] == "s":
                k = len(qs)
                ACT(F("ea" + H, 0, k * n), F(bk, 0, k * n), AF.Abs)
                ACT(eqs(qs[0], k), F("ea" + H, 0, k * n), AF.Relu, 1.0, -1.0)
            else:
                for i, q in enumerate(qs):
                    TT(eqs(q), D, F(bk, i * n, i * n + n), OP.is_equal)
        cdp, ctp = F(B[2], 0, n), F(B[2], n, 2 * n)
        ACT(bf(21), TL, AF.Sign, 2048.5)
        MM([(F(B[3], 240, 320), BD, bf(21))])
        rs = bf(6)
        ACT(rs, F(B[3], 240, 320), AF.Relu, -15.0, -1.0)
        for j, qs in enumerate(CH):
            MM([(cdp, F("I4096"), eqs(q)) for q in qs], j < 2, j > 0)
        for j, qs in enumerate(CH):
            MM([(ctp, Sq(q), eqs(q)) for q in qs], j < 2, j > 0)
        PH[0] = "x"
        d1 = f3(96, 176)
        TT(d1, D, cdp, OP.subtract)
        TS(off1, d1, -2048.0, OP.max, 2063.0, OP.add)
        ACT(F("X" + H), IND(clk, off1), AF.Copy)
        fl = bf(0)
        ACT(fl, d1, AF.Sign, 2047.5)
        cdb, ctb = bf(1), bf(2)
        ACT(bf(1, 2), F(B[2], 0, 2 * n), AF.Copy, 0.0, 1.0 / 4096)
        PH[0] = "m"
        zps, tlp = F(B[3], 400, 480), F(B[3], 320, 400)
        MM([(zps, ID, Z)])
        MM([(tlp, ID, TL)])
        for q in range(16):
            TT(F("mn" + H, q * n, q * n + n), F("Y" + H, q, G16, 16), zps, OP.min)
        Gp, scp, kbp = F(B[1], 0, n), F(B[0], 0, n), F(B[0], n, 2 * n)
        MM([(Gp, BD, Z)] + [(Gp, Sq(q), F("Y" + H, q, G16, 16)) for q in range(16)])
        for j, qs in enumerate(CH):
            MM([(scp, Sq(q), F("mn" + H, q * n, q * n + n)) for q in qs], j < 2, j > 0)
        PH[0] = "k"
        nk = f3(0, n)
        ACT(nk, scp, AF.Identity, F("lim"), 2.0)
        vt, vs, vb = f3(176, 272), f3(272, 368), f3(368, 464)
        VT(vt, f3(0, 96))
        SC(vs, F("segV"), vt, -1000000.0, OP.min, OP.max)
        VT(vb, vs)
        MM([(kbp, F("R15f"), f3(368, 448))])
        oh, far, fc = bf(3), bf(4), bf(5)
        TT(far, nk, Gp, OP.is_lt)
        TT(fc, far, ctp, OP.mult)
        TT(oh, nk, kbp, OP.is_equal)
        TT(ts, oh, tlp, OP.mult)
        lst = F(B[0], 160, 170)
        MM([(lst, Sq(r), F(m, 2 * n + r, 4 * n, 16)) for r in range(16)] + [(lst, BD, F("bia"))])
        PH[0] = "c"
        cp = F(B[1], n, 2 * n)
        MM([(cp, BD, fl), (cp, F("BDa"), fc), (cp, F("BDr"), rs)])
        nm1, sq, q0, nm2, nm3, abm = bf(7), bf(9), bf(10), bf(11), bf(12), bf(18)
        ACT(sq, cp, AF.Square, 32.5)
        ACT(q0, cp, AF.Abs, 2048.0, 128.0)
        ACT(nm1, cp, AF.Relu, -15.0, -1.0)
        ACT(nm2, cp, AF.Relu, 80.0)
        if not last:
            ACT(abm, cp, AF.Relu, -65536.0 * 80, -65536.0)
            TT(bf(8), cdp, abm, OP.is_gt)
            ACT(bf(22), bf(8), AF.Copy, 0.0, 1.0, F("ac", h, h + 1))
        ACT(nm3, sq, AF.Relu, -324.0)
        PH[0] = "l"
        sql = F(B[0], 170, 180)
        MM([(sql, Sq(r), F("bf" + H, 9 * n + r, 11 * n, 16)) for r in range(16)])
        TS(lu(0), F(B[0], 165, 170), 2064.0, OP.add)
        yk = bf(13)
        ACT(yk, IND(clk, lu(0)), AF.Copy)
        CP(F("li" + H, 0, 10), lst)
        TS(F("uv" + H), F("li" + H, 0, 10), 255, OP.bitwise_and)
        uu, v32 = F("uv" + H, 0, 5), F("uv" + H, 5, 10)
        TT(lf(0), v32, uu, OP.subtract)
        nu = lf(1)
        TS(nu, F(B[0], 170, 175), 5184.0, OP.is_gt)
        TT(F("pv", 5 * h, 5 * h + 5), v32, F(B[0], 175, 180), OP.max)
        TT(lf(2), lf(0), nu, OP.mult)
        TT(lf(3), lf(2), uu, OP.add)
        CP(lu(1), lf(3))
        cs, csD, csT = F("hf" + H), F("hf" + H, 0, n), F("hf" + H, n, 2 * n)
        TS(csD, IND(F("sct", 0, 256), lu(1)), -2048.0, OP.add)
        CP(csT, IND(F("stt"), lu(1)))
        PH[0] = "h"
        for e in range(2):
            for j, qs in enumerate(CH):
                bk = B[(j + e) % 2]
                for i, q in enumerate(qs):
                    o = F(bk, i * n, i * n + n)
                    MM([(o, Rq(q), F(m, e * n, e * n + n)), (o, F("NI"), F("hf" + H, e * n, e * n + n))])
                for i, q in enumerate(qs):
                    ACT(F("ab" + H, e * G16 + q, (e + 1) * G16, 16), F(bk, i * n, i * n + n), AF.Abs)
            SC(F("sm" + H, e * G16, (e + 1) * G16), F("segM", 0, G16), F("ab" + H, e * G16, (e + 1) * G16), 0.0, OP.max, OP.min)
        PH[0] = "d"
        dg, tg, t1p = F(B[2], 160, 240), F(B[2], 240, 320), F(B[3], 320, 400)
        MM([(dg, ID, D), (dg, N8, cdb), (dg, N8, nm1)])
        MM([(tg, ID, TL), (tg, F("N25"), ctb), (tg, N8, oh), (tg, N8, nm1)])
        MM([(t1p, ID, TL), (t1p, F("N25"), ctb), (t1p, N8, oh)])
        ACT(F("t1s", h * n, h * n + n), t1p, AF.Relu, 2048.0)
        km, kx = bf(14, 2), f3(464, 624)
        ACT(km, F(B[2], 160, 320), AF.Relu, 2048.0)
        TS(f3(464, 544), dg, -2048.0, OP.max)
        TS(f3(544, 624), tg, -2050.0, OP.max)
        PH[0] = "z"
        SC(F("tp" + H), F("seg0"), F("X" + H), 0.0, OP.mult, OP.max)
        zd, z1, z2, z4 = [F(B[3], i * n, i * n + n) for i in range(4)]
        MM([(zd, ID, Z), (zd, F("NI"), yk)])
        A2 = bf(19)
        ACT(A2, zd, AF.Abs)
        MM([(z1, F("HI"), yk), (z1, F("HI"), F("tp" + H, 15, G16, 16)), (z1, F("N512"), nm1)])
        MM([(z2, ID, A2), (z2, F("N512"), nm2)])
        MM([(z4, ID, Z), (z4, F("N512"), nm3)])
        ACT(f3(624, 704), z1, AF.Identity, -0.25)
        TT(f3(704, 784), f3(624, 704), z2, OP.max)
        TT(f3(784, 864), f3(704, 784), z4, OP.max)
        o = "out%d%d" % (t, h)
        zo = F("fin", 320 + h * n, 320 + h * n + n) if last else F(o, 160, 240)
        TS(zo, f3(784, 864), 8388608.0, OP.add, 8388608.0, OP.subtract)
        PH[0] = "r"
        hp, hd = F(B[0], 0, 2 * n), bf(16, 2)
        for e in range(2):
            x = F(B[0], e * n, e * n + n)
            MM([(x, ID, F("sm" + H, e * G16 + 15, (e + 1) * G16, 16)), (x, ID, nm1)])
        ACT(hd, hp, AF.Relu, 1.0, -1.0)
        rp = F(B[2], 320, 480)
        MM([(rp, ID, cs), (rp, N8, km), (rp, N8, hd)])
        if last:
            TT(f3(944, 1104), kx, rp, OP.max)
            TS(F("fin", h * n, h * n + n), f3(944, 1024), 2047.0, OP.add, -1.0, OP.max)
            TS(F("fin", 160 + h * n, 160 + h * n + n), f3(1024, 1104), 2047.0, OP.add, -1.0, OP.max)
        else:
            TT(F(o, 0, 160), kx, rp, OP.max)
            add("g", "send", (t, h), [F(o)], [], 200)
            add("n", "arrive", (t, h), [], [F("msg%d%d" % (t + 1, h), 0, 240)], 0, arr=(t + 1, h))

    def proofs(t):
        pb = "p7"
        TS(F("pvb"), F("pv"), 4096.0, OP.min)
        VB, lp, ll = F(pb, 0, NM), F(pb, NM, 2 * NM), F(pb, 488, 498)
        for r in range(16):
            MM([(F(pb, r, NM, 16), Rq(r), F("pvb"))])
        ACT(F("VBs"), VB, AF.Copy)
        TT(F("VL"), F("VBs"), F("LOW"), OP.max)
        TT(F("eb"), IND(F("pv"), F("co")), F("VL"), OP.is_equal)
        lst = [(lp, F("BD"), F("eb"))]
        a = 0
        for c in range(1, 10):
            TS(F("el", a, a + 16 * c), F("VBs", 0, 16 * c), F("pv", c, c + 1), OP.is_equal)
            lst.append((F(pb, NM, NM + 16 * c), F("BD"), F("el", a, a + 16 * c)))
            a += 16 * c
        MM(lst)
        ACT(F("lo"), lp, AF.Copy)
        MM([(ll, Sq(r), F("lo", r, NM, 16)) for r in range(16)])
        TS(F("l0"), ll, 0.5, OP.is_gt, 4096.0, OP.mult)
        TT(F("xa"), F("l0"), F("pv"), OP.add)
        TT(F("xa"), F("xa"), F("DUM"), OP.min)
        CP(F("sou"), F("xa"))
        CP(IND(F("sct"), F("sou")), F("t1s"))

    def count():
        pa = F("p7", 504, 505)
        MM([(pa, F("BDf"), F("ac", 0, 1)), (pa, F("BDf"), F("ac", 1, 2))])
        TT(F("As"), F("As"), pa, OP.add)
        TS(F("Am"), F("As"), 31, OP.bitwise_and)
        TS(F("lim"), F("Am"), 8.0, OP.mult, F("thc"), OP.add)

    for t in range(VIS):
        for h in range(NH):
            PH[1:] = [t, h]
            visit(t, h)
        PH[:] = ["A", t, 0]
        if t < VIS - 1:
            count()
        PH[:] = ["P", t, 0]
        proofs(t)
    PH[:] = ["E", 0, 0]
    TS(F("yso"), F("sct", 0, 256), -1.0, OP.add)
    add("y", "sto", [("yd", 0), ("yt", 160), ("yz", 320)], [F("fin")], [], 100, dma="wr0", lat=2500)
    add("y", "stys", None, [F("yso")], [], 50, dma="wr1", lat=2500)
    return ops


def _overlap(a, b):
    if a[0] != b[0] or a[1] >= b[2] or b[1] >= a[2]:
        return False
    return not (a[3] == b[3] and a[3] > 1 and (a[1] - b[1]) % a[3])


def _covers(a, b):
    return a[3] == 1 and a[1] <= b[1] and a[2] >= b[2] or a == b


def _deps(ops):
    hist = {}
    sends = {}
    for o in ops:
        dep = {}
        acc = [(x, False) for x in o["r"]] + [(x, True) for x in o["w"]]
        for (x, wr) in acc:
            psum = _W[x[0]] == "psum"
            for (y, ywr, yo) in hist.get(x[0], []):
                if yo is o:
                    continue
                same = yo["q"] == o["q"]
                if psum and not same:
                    dep[yo["id"]] = True
                elif psum and o["q"] == "t":
                    dep.setdefault(yo["id"], False)
                elif (wr or ywr) and _overlap(x, y):
                    need = (not same) or (ywr and o["q"] != "t")
                    dep[yo["id"]] = dep.get(yo["id"], False) or need
        for (x, wr) in acc:
            L = hist.setdefault(x[0], [])
            if wr:
                ps = _W[x[0]] == "psum"
                L[:] = [e for e in L if e[2] is o or not (_covers(x, e[0]) and (not ps or e[2]["q"] == o["q"]))]
            L.append((x, wr, o))
        if o["call"] == "send":
            sends[o["args"]] = o["id"]
        if o["call"] == "arrive":
            dep[sends[o["args"]]] = False
        o["dep"] = dep


LAT = {"x": 130.0, "own": 80.0, "arr": 3800.0, "fix": 20.0}
SCALE = 1.1


def _schedule(ops, seed=0):
    succ = [[] for _ in ops]
    for o in ops:
        for d in o["dep"]:
            succ[d].append(o["id"])

    def dly(a, b):
        if a["call"] == "send":
            return LAT["arr"] if b["call"] == "arrive" else 0.0
        if "dma" in a:
            return a["lat"]
        if not b["dep"][a["id"]]:
            return 0.0
        return LAT["own"] if a["q"] == b["q"] else LAT["x"]
    pri = [0.0] * len(ops)
    for o in reversed(ops):
        pri[o["id"]] = o["cost"] + max([pri[s] + dly(o, ops[s]) for s in succ[o["id"]]] + [0.0])
    pri = [p + BIAS.get((o["ph"][0], o["ph"][2]), 0.0) + BIAS.get(o["ph"][1:], 0.0) for p, o in zip(pri, ops)]
    left = [len(o["dep"]) for o in ops]
    rt = [0.0] * len(ops)
    ready, free, order, start, end = {}, {}, {}, [0.0] * len(ops), 0.0
    for o in ops:
        if not left[o["id"]]:
            ready.setdefault(o["q"], []).append(o["id"])
    for _ in range(len(ops)):
        best = None
        for q, L in ready.items():
            f = free.get(q, 0.0)
            for i in L:
                k = (rt[i] if q == "n" else max(f, rt[i]), -pri[i])
                if best is None or k < best[0]:
                    best = (k, q, i)
        (s, _p), q, i = best
        ready[q].remove(i)
        o = ops[i]
        e = s + o["cost"] + (0.0 if q == "n" else LAT["fix"])
        start[i] = s
        free[q] = e
        end = max(end, e)
        order.setdefault(q, []).append(i)
        for x in succ[i]:
            rt[x] = max(rt[x], e + dly(o, ops[x]))
            left[x] -= 1
            if not left[x]:
                ready.setdefault(ops[x]["q"], []).append(x)
    return end, seed, order, start


_CACHE = {}
SEMQ = {"v": "sv", "s": "ss", "t": "st_", "g": "sg"}


def _plan():
    if "p" in _CACHE:
        return _CACHE["p"]
    ops = _build()
    _deps(ops)
    for o in ops:
        o["cost"] *= SCALE
    end, _s, order, start = _schedule(ops)
    cnt = {}
    for q, L in order.items():
        for i in L:
            o = ops[i]
            o["start"] = start[i]
            if "dma" in o:
                o["tok"] = (o["dma"], 48 if o["call"] == "sto" else 16)
            elif o["call"] == "arrive":
                o["tok"] = ("arr%d%d" % o["arr"], None)
            elif o["call"] != "send":
                cnt[SEMQ[q]] = cnt.get(SEMQ[q], 0) + 1
                o["tok"] = (SEMQ[q], cnt[SEMQ[q]])
    known = {}
    for i in sorted((i for L in order.values() for i in L), key=lambda i: (ops[i]["start"], i)):
        o = ops[i]
        kn = known.setdefault(o["q"], {})
        w = {}
        for d in sorted((d for d, nd in o["dep"].items() if nd), key=lambda d: -ops[d]["start"]):
            s, v = ops[d]["tok"]
            if v is None:
                v = 1
            if kn.get(s, 0) >= v:
                continue
            w[s] = max(w.get(s, 0), v)
            for s2, v2 in list(ops[d]["kn"].items()) + [(s, v)]:
                kn[s2] = max(kn.get(s2, 0), v2)
        o["wait"] = sorted(w.items())
        o["kn"] = dict(kn)
    _CACHE["p"] = (ops, order, cnt, end)
    return _CACHE["p"]


def rank_program(g, core, T, topo):
    rank = T.rank_of(core)
    if rank is None:
        return
    ops, order, cnt, _end = _plan()
    hops = [1, 4, 2]
    eng = {"v": g.vector, "s": g.scalar, "t": g.tensor, "g": g, "y": g.sync}
    N = len(T.cores)
    arrn = [0] + [len(topo.engines(T.cores[(rank - hops[t]) % N], core)) for t in range(VIS - 1)]

    def ap(x):
        if not isinstance(x, tuple):
            return x
        if x[0] == "IND":
            return ap(x[1]).indirect(ap(x[2]))
        if x[3] == 1:
            return T[x[0]][:, x[1]:x[2]]
        return T[x[0]][:, x[1]:x[2]:x[3]]

    nsend = 0
    for q in ("y", "s", "v", "t", "g"):
        e = eng[q]
        for i in order[q]:
            o = ops[i]
            for s, v in o["wait"]:
                e.wait_ge(T.sem[s], arrn[int(s[3])] if s[:3] == "arr" else v)
            a, call = o["args"], o["call"]
            if call == "send":
                t, h = a
                dst = T.cores[(rank + hops[t]) % N]
                rid, pid = topo.addr(dst, core)
                g.remote_dma(T["msg%d%d" % (t + 1, h)][:, 0:240], T["out%d%d" % (t, h)][:], T.sem["arr%d%d" % (t + 1, h)], T.sem.snd, pid, rid, topo.mask(core, dst))
                nsend += len(topo.engines(core, dst))
                continue
            if call == "ld":
                e.dma_start(ap(a[0]), T[a[1]][:, :]).then_inc(T.sem[o["dma"]], 16)
                continue
            if call == "sto":
                for nm, c in a:
                    e.dma_start(T[nm][:, :], T.fin[:, c:c + NM]).then_inc(T.sem[o["dma"]], 16)
                continue
            if call == "stys":
                e.dma_start(T.ys[:, :], T.yso[:, :]).then_inc(T.sem[o["dma"]], 16)
                continue
            if call == "mm":
                lst, st, sp = a
                for k, (oo, l, r) in enumerate(lst):
                    ins = e.matmul(ap(oo), ap(l), ap(r), st and k == 0, sp and k == len(lst) - 1)
            elif call == "tt":
                ins = e.tensor_tensor(ap(a[0]), ap(a[1]), ap(a[2]), a[3])
            elif call == "ts":
                if a[5] is None:
                    ins = e.tensor_scalar(ap(a[0]), ap(a[1]), ap(a[2]), None, a[4])
                else:
                    ins = e.tensor_scalar(ap(a[0]), ap(a[1]), ap(a[2]), ap(a[3]), a[4], a[5])
            elif call == "cp":
                ins = e.tensor_copy(ap(a[0]), ap(a[1]))
            elif call == "ms":
                ins = e.memset(ap(a[0]), a[1])
            elif call == "sc":
                ins = e.tensor_tensor_scan(ap(a[0]), ap(a[1]), ap(a[2]), a[3], a[4], a[5])
            elif call == "vt":
                ins = e.transpose(ap(a[0]), ap(a[1]))
            elif call == "act":
                kw = {} if a[5] is None else {"accum_out": ap(a[5])}
                ins = e.activation(ap(a[0]), ap(a[1]), a[2], ap(a[3]), ap(a[4]), **kw)
            elif call == "iota":
                ins = e.iota(ap(a[0]), a[1], a[2], a[3], allow_small_or_imprecise_dtypes=True)
            elif call == "asel":
                ins = e.affine_select(ap(a[0]), ap(a[0]), a[1], OP.not_equal, a[2], 0, 0)
            ins.then_inc(T.sem[o["tok"][0]], 1)
    g.wait_ge(T.sem.snd, nsend)
    for s, v in sorted(cnt.items()):
        g.wait_ge(T.sem[s], v)
    g.wait_ge(T.sem.wr0, 48)
    g.wait_ge(T.sem.wr1, 16)
